import numpy as np
import ml_dtypes


def mxq(x, axis, fmt="e4m3"):
    dtype, down = {"e4m3": (ml_dtypes.float8_e4m3fn, 7), "e5m2": (ml_dtypes.float8_e5m2, 14)}[fmt]
    v = np.moveaxis(np.asarray(x, np.float32).astype(ml_dtypes.bfloat16).astype(np.float64), axis, -1)
    blocks = v.reshape(v.shape[:-1] + (-1, 32))
    amax = np.abs(blocks).max(-1, keepdims=True)
    byte = np.maximum(np.where(amax > 0, np.frexp(amax)[1] - 1 + 127, 0) - down, 1)
    scale = np.exp2(byte - 127.0)
    codes = (blocks / scale).astype(np.float32).astype(dtype).astype(np.float64)
    return np.moveaxis((codes * scale).reshape(v.shape), -1, axis)


WIDE = False


def mx_kscale(k):
    if not WIDE:
        return np.ones(k)
    levels = np.array([10, -10, 5, -5, 0])
    if k % 512:
        return np.exp2(np.random.permutation(np.resize(levels, k // 32))).repeat(32)
    a = np.empty((k // 512, 16))
    for p in range(k // 512):
        a[p, :8] = np.random.permutation(np.resize(levels, 8))
        for g in range(8):
            far = levels[np.abs(levels - a[p, g]) >= 10]
            a[p, g + 8] = far[np.random.randint(len(far))]
    return np.exp2(a.ravel()).repeat(32)


def f64(x):
    return np.asarray(x).astype(np.float64)


def striped(idx):
    return np.tile(idx.reshape(-1, 16).T, (8, 1)).astype(np.uint16)


def unstriped(offs):
    return offs[:16].T.reshape(-1).astype(np.int64)


E2M1 = np.array([0.0, 0.5, 1.0, 1.5, 2.0, 3.0, 4.0, 6.0, -0.0, -0.5, -1.0, -1.5, -2.0, -3.0, -4.0, -6.0])


def pack_weight(w, fmt):
    k, n = w.shape
    w = f64(np.asarray(w, np.float32).astype(ml_dtypes.bfloat16)).reshape(k // 32, 32, n)
    amax = np.abs(w).max(1)
    if fmt == "e4m3":
        byte = np.frexp(amax)[1] - 1 + 127 - 7
    else:
        mant, ex = np.frexp(amax / 6.0)
        byte = np.where(mant > 0.5, ex, ex - 1) + 127
    byte = np.clip(np.where(amax > 0, byte, 1), 1, 254)
    scaled = (w * np.exp2(127.0 - byte)[:, None, :]).reshape(k, n).astype(np.float32)
    by_word = np.ascontiguousarray(scaled.reshape(k // 512, 128, 4, n).transpose(0, 1, 3, 2))
    if fmt == "e4m3":
        words = by_word.astype(ml_dtypes.float8_e4m3fn).view(np.uint8)
    else:
        c = by_word.astype(ml_dtypes.float4_e2m1fn).view(np.uint8) & 0xF
        words = (c[..., 0::2] | (c[..., 1::2] << 4)).reshape(k // 512, 128, 2 * n)
    return np.ascontiguousarray(words), np.ascontiguousarray(byte.astype(np.uint8).reshape(k // 512, 16, n))


def unpack_weight(words, scales, fmt):
    g, _, n = scales.shape
    words = np.ascontiguousarray(words).reshape(g, 128, n, -1)
    if fmt == "e4m3":
        vals = words.view(ml_dtypes.float8_e4m3fn).astype(np.float64)
    else:
        nib = np.empty((g, 128, n, 4), np.uint8)
        nib[..., 0::2] = words & 0xF
        nib[..., 1::2] = words >> 4
        vals = E2M1[nib]
    vals = vals * np.repeat(np.exp2(scales.astype(np.float64) - 127.0), 8, axis=1)[..., None]
    return vals.transpose(0, 1, 3, 2).reshape(g * 512, n)


def gelu(v):
    return 0.5 * v * (1.0 + np.tanh(np.sqrt(2.0 / np.pi) * (v + 0.044715 * v**3)))


def striped8(idx):
    return np.concatenate([v.reshape(-1, 16).T for v in idx]).astype(np.uint16)


def unstriped8(offs):
    return np.stack([offs[16 * g:16 * g + 16].T.reshape(-1) for g in range(8)]).astype(np.int64)


def heads(xT, wgt, idx8):
    k = np.arange(xT.shape[0])
    return wgt[k // 4 % 128] * xT[k[:, None], idx8[k % 512 // 64]]


K, T, S, H, N, G, P = 1024, 2048, 1024, 512, 512, 8, 128

def setup_inputs():
    n = np.random.standard_normal
    s = mx_kscale(K)[:, None]
    u = mx_kscale(H)[:, None]
    w2_words, w2_scales = pack_weight(0.75 * n((K, H)) / np.sqrt(K) / s, "e2m1")
    w4_words, w4_scales = pack_weight(n((H, N)) / np.sqrt(H) / u, "e4m3")
    lists = np.stack([np.random.permutation(T)[:S] for _ in range(G)])
    return {
        "xT": (n((K, T)) * s).astype(np.float32),
        "wgt": np.repeat(np.random.uniform(0.5, 2.0, (G, S)), P // G, axis=0).astype(np.float32),
        "offs": striped8(lists),
        "w1": (0.75 * n((K, H)) / np.sqrt(K) / s * u.T).astype(np.float32),
        "w2_words": w2_words, "w2_scales": w2_scales,
        "w3": (0.75 * n((K, H)) / np.sqrt(K) / s).astype(np.float32),
        "b3": (0.5 * n(H)).astype(np.float32),
        "w4_words": w4_words, "w4_scales": w4_scales,
        "b4": (0.5 * n(N)).astype(np.float32),
    }

def reference(xT, wgt, offs, w1, w2_words, w2_scales, w3, b3, w4_words, w4_scales, b4):
    xg = heads(f64(xT), f64(wgt), unstriped8(offs))
    xq = mxq(xg, 0, "e4m3")
    w2 = unpack_weight(w2_words, w2_scales, "e2m1")
    w4 = unpack_weight(w4_words, w4_scales, "e4m3")
    a = mxq(f64(w1), 0, "e4m3").T @ xq
    b = w2.T @ xq
    c = mxq(f64(w3), 0, "e4m3").T @ xq
    h = a * b * (c + f64(b3)[:, None])
    e = w4.T @ mxq(h, 0, "e4m3")
    return e + f64(b4)[:, None]

@@ -1,0 +1,256 @@
+from contextlib import ExitStack
+
+import concourse.mybir as mybir
+
+K, T, S, H, N = 1024, 2048, 1024, 512, 512
+FLOPS = 2 * S * (3 * K * H + H * N)
+
+F32 = mybir.dt.float32
+BF16 = mybir.dt.bfloat16
+I32 = mybir.dt.int32
+U32 = mybir.dt.uint32
+U16 = mybir.dt.uint16
+U8 = mybir.dt.uint8
+FP8X4 = mybir.dt.float8_e4m3fn_x4
+FP4X4 = mybir.dt.float4_e2m1fn_x4
+MULT = mybir.AluOpType.mult
+ADD = mybir.AluOpType.add
+IDENT = mybir.ActivationFunctionType.Identity
+
+P = 128
+UNITS = [512,256,256]
+ECH = [[256,256],[128,128],[128,128]]
+LOADS = ["offs","w2","g0","g1","x4","s2","g2","x2","x6","x5","x7","x1","x3","x0","w30","s4","w31","w10","b3","w111","b4","w4","w110"]
+PROG = [["W","w3",0],["F",1,0],["F",0,0],["F",2,1],["P"],["F",1,1],["b",1],["W","w3",1],["F",0,1],["b",0],["c",0],["W","w1",1],["W","w1",0],["c",1],["a",0],["F",2,0],["a",1],["b",2],["c",2],["a",2]]
+VCAST = ["w111","w310","x00","x20"]
+GCAST = []
+NB = [2,2,2,2]
+
+
+def tile_list_triplet_contact_energy_kernel(
+    tc, xT, wgt, offs, w1, w2_words, w2_scales, w3, b3, w4_words, w4_scales, b4, out
+):
+    nc = tc.nc
+    with ExitStack() as ctx:
+        keep = ctx.enter_context(tc.tile_pool(name="keep", bufs=1))
+        ring = ctx.enter_context(tc.tile_pool(name="ring", bufs=3))
+        psum = ctx.enter_context(tc.psum_pool(name="psum", bufs=2))
+
+        lists = keep.tile([P, S // 16], U16, name="lists")
+        weights = keep.tile([P, S], F32, name="weights")
+        planes = [keep.tile([P, T], F32, name="plane%d" % i) for i in range(8)]
+        w_raw = {(w, a): keep.tile([P, 4, H], F32, name="raw_%s_%d" % (w, a)) for w in ("w1", "w3") for a in range(2)}
+        w2_raw = keep.tile([P, 2, 2 * H], U8, name="w2_raw")
+        given_scales = keep.tile([P, 3, H], U8, name="given_scales", align_bytes=64)
+        w4_codes = keep.tile([P, N], U32, name="w4_codes", align_bytes=64)
+        b3_cols = keep.tile([P, 4], F32, name="b3_cols")
+        b4_cols = keep.tile([P, 4], F32, name="b4_cols")
+        w2_codes = keep.tile([P, 2, 2 * H], U8, name="w2_codes", align_bytes=64)
+        w2_planes = keep.tile([P, 2, H], U8, name="w2_planes", align_bytes=64)
+
+        nc.vector.memset(given_scales[:].bitcast(U32), 0)
+        src_w = {"w1": w1, "w3": w3}
+        for name in LOADS:
+            if name == "offs":
+                nc.sync.dma_start(lists[:], offs)
+            elif name[0] == "g":
+                lo, hi = [(0, 256), (256, 512), (512, 1024)][int(name[1])]
+                nc.sync.dma_start(out=weights[:, lo:hi], in_=wgt[:, lo:hi])
+            elif name[0] == "x":
+                a, i = divmod(int(name[1]), 4)
+                rows = xT[512 * a : 512 * (a + 1), :].rearrange("(p i) t -> p i t", i=4)
+                nc.sync.dma_start(out=planes[4 * a + i][:], in_=rows[:, i, :])
+            elif name == "w2":
+                nc.sync.dma_start(out=w2_raw[:].bitcast(I32), in_=w2_words.rearrange("a p n -> p a n").bitcast(I32))
+            elif name == "s2":
+                for q in range(4):
+                    nc.sync.dma_start(
+                        out=given_scales[32 * q : 32 * q + 4, 0:2, :].bitcast(I32),
+                        in_=w2_scales[:, 4 * q : 4 * q + 4, :].rearrange("a q e -> q a e").bitcast(I32),
+                    )
+            elif name == "s4":
+                for q in range(4):
+                    nc.sync.dma_start(
+                        out=given_scales[32 * q : 32 * q + 4, 2, :].bitcast(I32),
+                        in_=w4_scales[0, 4 * q : 4 * q + 4, :].bitcast(I32),
+                    )
+            elif name == "w4":
+                nc.sync.dma_start(
+                    out=w4_codes[:].bitcast(I32), in_=w4_words[0].rearrange("p n t -> p (n t)").bitcast(I32)
+                )
+            elif name == "b3":
+                nc.sync.dma_start(out=b3_cols[:], in_=b3.rearrange("(p t) -> p t", t=4))
+            elif name == "b4":
+                with nc.allow_non_contiguous_dma(reason="one bias value a partition and output tile"):
+                    nc.sync.dma_start(out=b4_cols[:], in_=b4.rearrange("(c p) -> p c", p=P))
+            else:
+                w, a = name[:2], int(name[2])
+                rows = src_w[w][512 * a : 512 * (a + 1), :].rearrange("(p j) c -> p j c", j=4)
+                if len(name) == 3:
+                    nc.sync.dma_start(out=w_raw[w, a][:], in_=rows)
+                else:
+                    cols = slice(256 * int(name[3]), 256 * int(name[3]) + 256)
+                    nc.sync.dma_start(out=w_raw[w, a][:, :, cols], in_=rows[:, :, cols])
+
+        w_codes = {}
+        w_scales = {}
+        x_codes = {}
+        x_scales = {}
+        b_sb = {}
+        bc_sb = {}
+
+        def permute_w2():
+            for a in range(2):
+                nc.vector.tensor_copy(
+                    out=w2_codes[:, a, :].rearrange("p (t m b) -> p t m b", t=4, b=2),
+                    in_=w2_raw[:, a, :].rearrange("p (m t b) -> p t m b", t=4, b=2),
+                )
+            nc.vector.tensor_copy(
+                out=w2_planes[:].rearrange("p a (t m) -> p a t m", t=4),
+                in_=given_scales[:, 0:2, :].rearrange("p a (m t) -> p a t m", t=4),
+            )
+
+        def quantize_weight(w, a):
+            grouped = keep.tile([P, 4 * H], BF16, name="grouped_%s_%d" % (w, a), align_bytes=64)
+            for half in range(2):
+                dst = grouped[:].rearrange("p (t m j) -> p m j t", t=4, j=4)[:, 64 * half : 64 * half + 64]
+                src = w_raw[w, a][:].rearrange("p j (m t) -> p m j t", t=4)[:, 64 * half : 64 * half + 64]
+                key = "%s%d%d" % (w, a, half)
+                if key in VCAST:
+                    nc.vector.tensor_copy(out=dst, in_=src)
+                elif key in GCAST:
+                    nc.gpsimd.tensor_scalar(out=dst, in0=src, scalar1=1.0, scalar2=0.0, op0=MULT, op1=ADD)
+                else:
+                    nc.scalar.copy(out=dst, in_=src)
+            w_codes[w, a] = keep.tile([P, H], U32, name="codes_%s_%d" % (w, a), align_bytes=64)
+            w_scales[w, a] = keep.tile([P, H], U8, name="scales_%s_%d" % (w, a), align_bytes=64)
+            nc.vector.quantize_mx(out=w_codes[w, a][:].bitcast(FP8X4), scales=w_scales[w, a][:], in_=grouped[:])
+
+        def gather(u, a):
+            n, s0 = UNITS[u], sum(UNITS[:u])
+            picked = keep.tile([P, 4, n], F32, name="picked_%d_%d" % (u, a))
+            for i in range(4):
+                nc.vector.tensor_tensor(
+                    picked[:, i, :],
+                    planes[4 * a + i][:].indirect(lists[:, s0 // 16 : (s0 + n) // 16]),
+                    weights[:, s0 : s0 + n],
+                    MULT,
+                )
+            grouped = keep.tile([P, 4 * n], BF16, name="x_grouped_%d_%d" % (u, a), align_bytes=64)
+            dst = grouped[:].rearrange("p (c i t) -> p c t i", i=4, t=4)
+            src = picked[:].rearrange("p t (c i) -> p c t i", i=4)
+            if "x%d%d" % (u, a) in VCAST:
+                nc.vector.tensor_copy(out=dst, in_=src)
+            else:
+                nc.scalar.copy(out=dst, in_=src)
+            x_codes[u, a] = keep.tile([P, n], U32, name="x_codes_%d_%d" % (u, a), align_bytes=64)
+            x_scales[u, a] = keep.tile([P, n], U8, name="x_scales_%d_%d" % (u, a), align_bytes=64)
+            nc.vector.quantize_mx(out=x_codes[u, a][:].bitcast(FP8X4), scales=x_scales[u, a][:], in_=grouped[:])
+
+        def product(w, u, t, cols, acc):
+            m = slice(128 * t, 128 * t + 128)
+            for a in range(2):
+                if w == "w2":
+                    lhs = w2_codes[:, a, 256 * t : 256 * t + 256].bitcast(FP4X4)
+                    lhs_scale = w2_planes[:, a, m]
+                else:
+                    lhs = w_codes[w, a][:, m].bitcast(FP8X4)
+                    lhs_scale = w_scales[w, a][:, m]
+                nc.tensor.matmul_mx(
+                    out=acc,
+                    lhsT=lhs,
+                    lhsT_scale=lhs_scale,
+                    rhs=x_codes[u, a][:, cols].bitcast(FP8X4),
+                    rhs_scale=x_scales[u, a][:, cols],
+                    start=(a == 0),
+                    stop=(a == 1),
+                )
+
+        def stage_b(u):
+            n = UNITS[u]
+            b_sb[u] = keep.tile([P, 4, n], F32, name="b_sb_%d" % u)
+            w = 512 if n == 512 else 128
+            per = 512 // w
+            for c0 in range(0, n, w):
+                for g in range(4 // per):
+                    acc = psum.tile([P, per, w], F32, name="acc_b", bufs=NB[0])
+                    for t in range(per):
+                        product("w2", u, g * per + t, slice(c0, c0 + w), acc[:, t, :])
+                    nc.scalar.copy(out=b_sb[u][:, g * per : (g + 1) * per, c0 : c0 + w], in_=acc[:])
+
+        def stage_c(u):
+            n = UNITS[u]
+            bc_sb[u] = b_sb[u]
+            per = 512 // n
+            for g in range(4 // per):
+                acc = psum.tile([P, per, n], F32, name="acc_c", bufs=NB[1])
+                for t in range(per):
+                    product("w3", u, g * per + t, slice(0, n), acc[:, t, :])
+                for t in range(per):
+                    tt = g * per + t
+                    nc.vector.scalar_tensor_tensor(
+                        out=bc_sb[u][:, tt, :],
+                        in0=acc[:, t, :],
+                        scalar=b3_cols[:, tt : tt + 1],
+                        in1=b_sb[u][:, tt, :],
+                        op0=ADD,
+                        op1=MULT,
+                    )
+
+        def stage_a(u):
+            n, s0 = UNITS[u], sum(UNITS[:u])
+            c0 = 0
+            for ec in ECH[u]:
+                h = ring.tile([P, 4 * ec], BF16, name="h", align_bytes=64)
+                for c in range(ec // 128):
+                    cols = slice(c0 + 128 * c, c0 + 128 * c + 128)
+                    acc = psum.tile([P, 4, 128], F32, name="acc_a", bufs=NB[2])
+                    for t in range(4):
+                        product("w1", u, t, cols, acc[:, t, :])
+                    nc.vector.tensor_tensor(
+                        h[:, 512 * c : 512 * c + 512].rearrange("p (c i t) -> p c t i", i=4, t=4),
+                        acc[:].rearrange("p t (c i) -> p c t i", i=4),
+                        bc_sb[u][:, :, cols].rearrange("p t (c i) -> p c t i", i=4),
+                        MULT,
+                    )
+                h_codes = ring.tile([P, ec], U32, name="h_codes", align_bytes=64)
+                h_scales = ring.tile([P, ec], U8, name="h_scales", align_bytes=64)
+                nc.vector.quantize_mx(out=h_codes[:].bitcast(FP8X4), scales=h_scales[:], in_=h[:])
+                result = ring.tile([P, 4, ec], F32, name="result")
+                per = 512 // ec
+                for g in range(4 // per):
+                    acc = psum.tile([P, per, ec], F32, name="acc_e", bufs=NB[3])
+                    for t in range(per):
+                        m = slice(128 * (g * per + t), 128 * (g * per + t) + 128)
+                        nc.tensor.matmul_mx(
+                            out=acc[:, t, :],
+                            lhsT=w4_codes[:, m].bitcast(FP8X4),
+                            lhsT_scale=given_scales[:, 2, m],
+                            rhs=h_codes[:].bitcast(FP8X4),
+                            rhs_scale=h_scales[:],
+                            start=True,
+                            stop=True,
+                        )
+                    for t in range(per):
+                        tt = g * per + t
+                        nc.scalar.activation(
+                            out=result[:, tt, :], in_=acc[:, t, :], func=IDENT, bias=b4_cols[:, tt : tt + 1]
+                        )
+                nc.sync.dma_start(
+                    out=out[:, s0 + c0 : s0 + c0 + ec].rearrange("(c p) j -> p c j", p=P), in_=result[:]
+                )
+                c0 += ec
+
+        for step in PROG:
+            if step[0] == "P":
+                permute_w2()
+            elif step[0] == "W":
+                quantize_weight(step[1], step[2])
+            elif step[0] == "F":
+                gather(step[1], step[2])
+            elif step[0] == "b":
+                stage_b(step[1])
+            elif step[0] == "c":
+                stage_c(step[1])
+            else:
+                stage_a(step[1])

@@ -18,13 +18,16 @@ ADD = mybir.AluOpType.add
 IDENT = mybir.ActivationFunctionType.Identity
 
 P = 128
-UNITS = [512,256,256]
-ECH = [[256,256],[128,128],[128,128]]
-LOADS = ["offs","w2","g0","g1","x4","s2","g2","x2","x6","x5","x7","x1","x3","x0","w30","s4","w31","w10","b3","w111","b4","w4","w110"]
-PROG = [["W","w3",0],["F",1,0],["F",0,0],["F",2,1],["P"],["F",1,1],["b",1],["W","w3",1],["F",0,1],["b",0],["c",0],["W","w1",1],["W","w1",0],["c",1],["a",0],["F",2,0],["a",1],["b",2],["c",2],["a",2]]
-VCAST = ["w111","w310","x00","x20"]
+UNITS = [512,512]
+REUSE = {"x01":"x00"}
+Q2 = []
+SPLIT = ["e10","e11","x11"]
+KORDER = {"a":[0,1],"b":[0,1],"c":[0,1]}
+LOADS = ["s2","w2","offs","x3","g0","g1","x7","x0","x2","x1","x6","x4","w31","x5","w111","w30","w110","b3","w10","w4","s4","b4"]
+PROG = [["G",0,1],["C","w1",0,1],["G",0,4],["G",0,5],["C","w3",1,0],["G",1,5],["G",1,7],["G",0,6],["C","w1",1,0],["G",0,7],["C","w1",1,1],["G",1,6],["C","w3",0,1],["C","w1",0,0],["G",0,0],["G",0,2],["G",1,1],["G",1,3],["P"],["G",0,3],["X",0,0,0],["G",1,4],["G",1,0],["G",1,2],["X",0,0,1],["Q",0,0,1],["X",0,1,0],["X",1,0,0],["W","w1",1],["X",0,1,1],["C","w3",0,0],["W","w1",0],["Q",0,1,1],["X",1,0,1],["bm",0,0],["X",1,1,0],["W","w3",0],["Q",1,0,1],["bm",0,3],["bm",0,1],["C","w3",1,1],["bm",0,2],["W","w3",1],["b",0,0],["X",1,1,1],["Q",1,1,0],["Q",1,1,1],["b",0,1],["cm",0,3],["b",0,3],["bm",1,1],["bm",1,2],["b",0,2],["cm",0,2],["c",0,3],["cm",0,1],["cm",0,0],["b",1,1],["Am",0,1],["cm",1,2],["c",0,2],["cm",1,1],["b",1,2],["c",0,1],["c",0,0],["c",1,2],["Am",0,2],["Am",0,0],["Am",0,3],["bm",1,3],["A",0,3],["A",0,1],["bm",1,0],["A",0,0],["b",1,0],["c",1,1],["cm",1,3],["Eq",0,1],["A",0,2],["Em",0,1,0],["Em",0,1,1],["cm",1,0],["Am",1,0],["Am",1,1],["b",1,3],["Eo",0,1,0],["c",1,3],["c",1,0],["Eq",0,3],["Em",0,3,0],["A",1,0],["Eo",0,3,0],["Em",0,3,1],["Am",1,2],["Am",1,3],["A",1,3],["A",1,1],["A",1,2],["Eq",1,1],["Eo",0,1,1],["Eo",0,3,1],["Es",0,1],["Eq",1,0],["Em",1,0,0],["Eq",1,3],["Em",1,1,0],["Es",0,3],["Eo",1,1,0],["Eo",1,0,0],["Em",1,3,0],["Es",1,0],["Eo",1,3,0],["Eq",1,2],["Em",1,2,0],["Es",1,1],["Eo",1,2,0],["Es",1,2],["Es",1,3]]
+VCAST = ["o101","o110","o111","o120","o130","w110","w300","w301","x010"]
 GCAST = []
-NB = [2,2,2,2]
+NB = [8]
 
 
 def tile_list_triplet_contact_energy_kernel(
@@ -33,8 +36,7 @@ def tile_list_triplet_contact_energy_kernel(
     nc = tc.nc
     with ExitStack() as ctx:
         keep = ctx.enter_context(tc.tile_pool(name="keep", bufs=1))
-        ring = ctx.enter_context(tc.tile_pool(name="ring", bufs=3))
-        psum = ctx.enter_context(tc.psum_pool(name="psum", bufs=2))
+        psum = ctx.enter_context(tc.psum_pool(name="psum", bufs=1))
 
         lists = keep.tile([P, S // 16], U16, name="lists")
         weights = keep.tile([P, S], F32, name="weights")
@@ -51,46 +53,47 @@ def tile_list_triplet_contact_energy_kernel(
         nc.vector.memset(given_scales[:].bitcast(U32), 0)
         src_w = {"w1": w1, "w3": w3}
         for name in LOADS:
+            queue = nc.scalar if name in Q2 else nc.sync
             if name == "offs":
                 nc.sync.dma_start(lists[:], offs)
             elif name[0] == "g":
-                lo, hi = [(0, 256), (256, 512), (512, 1024)][int(name[1])]
-                nc.sync.dma_start(out=weights[:, lo:hi], in_=wgt[:, lo:hi])
+                lo, hi = [(0, 512), (512, 1024)][int(name[1])]
+                queue.dma_start(out=weights[:, lo:hi], in_=wgt[:, lo:hi])
             elif name[0] == "x":
                 a, i = divmod(int(name[1]), 4)
                 rows = xT[512 * a : 512 * (a + 1), :].rearrange("(p i) t -> p i t", i=4)
-                nc.sync.dma_start(out=planes[4 * a + i][:], in_=rows[:, i, :])
+                queue.dma_start(out=planes[4 * a + i][:], in_=rows[:, i, :])
             elif name == "w2":
-                nc.sync.dma_start(out=w2_raw[:].bitcast(I32), in_=w2_words.rearrange("a p n -> p a n").bitcast(I32))
+                queue.dma_start(out=w2_raw[:].bitcast(I32), in_=w2_words.rearrange("a p n -> p a n").bitcast(I32))
             elif name == "s2":
                 for q in range(4):
-                    nc.sync.dma_start(
+                    queue.dma_start(
                         out=given_scales[32 * q : 32 * q + 4, 0:2, :].bitcast(I32),
                         in_=w2_scales[:, 4 * q : 4 * q + 4, :].rearrange("a q e -> q a e").bitcast(I32),
                     )
             elif name == "s4":
                 for q in range(4):
-                    nc.sync.dma_start(
+                    queue.dma_start(
                         out=given_scales[32 * q : 32 * q + 4, 2, :].bitcast(I32),
                         in_=w4_scales[0, 4 * q : 4 * q + 4, :].bitcast(I32),
                     )
             elif name == "w4":
-                nc.sync.dma_start(
+                queue.dma_start(
                     out=w4_codes[:].bitcast(I32), in_=w4_words[0].rearrange("p n t -> p (n t)").bitcast(I32)
                 )
             elif name == "b3":
-                nc.sync.dma_start(out=b3_cols[:], in_=b3.rearrange("(p t) -> p t", t=4))
+                queue.dma_start(out=b3_cols[:], in_=b3.rearrange("(p t) -> p t", t=4))
             elif name == "b4":
                 with nc.allow_non_contiguous_dma(reason="one bias value a partition and output tile"):
-                    nc.sync.dma_start(out=b4_cols[:], in_=b4.rearrange("(c p) -> p c", p=P))
+                    queue.dma_start(out=b4_cols[:], in_=b4.rearrange("(c p) -> p c", p=P))
             else:
                 w, a = name[:2], int(name[2])
                 rows = src_w[w][512 * a : 512 * (a + 1), :].rearrange("(p j) c -> p j c", j=4)
                 if len(name) == 3:
-                    nc.sync.dma_start(out=w_raw[w, a][:], in_=rows)
+                    queue.dma_start(out=w_raw[w, a][:], in_=rows)
                 else:
                     cols = slice(256 * int(name[3]), 256 * int(name[3]) + 256)
-                    nc.sync.dma_start(out=w_raw[w, a][:, :, cols], in_=rows[:, :, cols])
+                    queue.dma_start(out=w_raw[w, a][:, :, cols], in_=rows[:, :, cols])
 
         w_codes = {}
         w_scales = {}
@@ -110,46 +113,79 @@ def tile_list_triplet_contact_energy_kernel(
                 in_=given_scales[:, 0:2, :].rearrange("p a (m t) -> p a t m", t=4),
             )
 
-        def quantize_weight(w, a):
-            grouped = keep.tile([P, 4 * H], BF16, name="grouped_%s_%d" % (w, a), align_bytes=64)
-            for half in range(2):
-                dst = grouped[:].rearrange("p (t m j) -> p m j t", t=4, j=4)[:, 64 * half : 64 * half + 64]
-                src = w_raw[w, a][:].rearrange("p j (m t) -> p m j t", t=4)[:, 64 * half : 64 * half + 64]
-                key = "%s%d%d" % (w, a, half)
-                if key in VCAST:
-                    nc.vector.tensor_copy(out=dst, in_=src)
-                elif key in GCAST:
-                    nc.gpsimd.tensor_scalar(out=dst, in0=src, scalar1=1.0, scalar2=0.0, op0=MULT, op1=ADD)
-                else:
-                    nc.scalar.copy(out=dst, in_=src)
-            w_codes[w, a] = keep.tile([P, H], U32, name="codes_%s_%d" % (w, a), align_bytes=64)
-            w_scales[w, a] = keep.tile([P, H], U8, name="scales_%s_%d" % (w, a), align_bytes=64)
-            nc.vector.quantize_mx(out=w_codes[w, a][:].bitcast(FP8X4), scales=w_scales[w, a][:], in_=grouped[:])
+        w_grouped = {}
+        picked = {}
+        x_grouped = {}
+        h_tiles = {}
+        staged = {}
+        for key in ("x00", "x01", "x10", "x11", "w30", "w31", "w10", "w11"):
+            if key not in REUSE:
+                staged[key] = keep.tile([P, 2048], BF16, name="staged_" + key, align_bytes=64)
+        for rounds in range(8):
+            for key in REUSE:
+                if REUSE[key] in staged:
+                    staged[key] = staged[REUSE[key]]
+        for key in w_raw:
+            w_grouped[key] = staged["%s%d" % key]
+            w_codes[key] = keep.tile([P, H], U32, name="codes_%s_%d" % key, align_bytes=64)
+            w_scales[key] = keep.tile([P, H], U8, name="scales_%s_%d" % key, align_bytes=64)
+        for u in range(2):
+            b_sb[u] = keep.tile([P, 4, 512], F32, name="b_sb_%d" % u)
+            h_tiles[u] = keep.tile([P, 2048], BF16, name="h_%d" % u, align_bytes=64)
+            for a in range(2):
+                picked[u, a] = keep.tile([P, 4, 512], F32, name="picked_%d_%d" % (u, a))
+                x_grouped[u, a] = staged["x%d%d" % (u, a)]
+                x_codes[u, a] = keep.tile([P, 512], U32, name="x_codes_%d_%d" % (u, a), align_bytes=64)
+                x_scales[u, a] = keep.tile([P, 512], U8, name="x_scales_%d_%d" % (u, a), align_bytes=64)
 
-        def gather(u, a):
-            n, s0 = UNITS[u], sum(UNITS[:u])
-            picked = keep.tile([P, 4, n], F32, name="picked_%d_%d" % (u, a))
-            for i in range(4):
-                nc.vector.tensor_tensor(
-                    picked[:, i, :],
-                    planes[4 * a + i][:].indirect(lists[:, s0 // 16 : (s0 + n) // 16]),
-                    weights[:, s0 : s0 + n],
-                    MULT,
-                )
-            grouped = keep.tile([P, 4 * n], BF16, name="x_grouped_%d_%d" % (u, a), align_bytes=64)
-            dst = grouped[:].rearrange("p (c i t) -> p c t i", i=4, t=4)
-            src = picked[:].rearrange("p t (c i) -> p c t i", i=4)
-            if "x%d%d" % (u, a) in VCAST:
+        def cast(key, dst, src):
+            if key in VCAST:
                 nc.vector.tensor_copy(out=dst, in_=src)
+            elif key in GCAST:
+                nc.gpsimd.tensor_scalar(out=dst, in0=src, scalar1=1.0, scalar2=0.0, op0=MULT, op1=ADD)
             else:
                 nc.scalar.copy(out=dst, in_=src)
-            x_codes[u, a] = keep.tile([P, n], U32, name="x_codes_%d_%d" % (u, a), align_bytes=64)
-            x_scales[u, a] = keep.tile([P, n], U8, name="x_scales_%d_%d" % (u, a), align_bytes=64)
-            nc.vector.quantize_mx(out=x_codes[u, a][:].bitcast(FP8X4), scales=x_scales[u, a][:], in_=grouped[:])
 
-        def product(w, u, t, cols, acc):
+        def cast_weight(w, a, half):
+            dst = w_grouped[w, a][:].rearrange("p (t m j) -> p m j t", t=4, j=4)[:, 64 * half : 64 * half + 64]
+            src = w_raw[w, a][:].rearrange("p j (m t) -> p m j t", t=4)[:, 64 * half : 64 * half + 64]
+            cast("%s%d%d" % (w, a, half), dst, src)
+
+        def quantize_weight(w, a):
+            nc.vector.quantize_mx(
+                out=w_codes[w, a][:].bitcast(FP8X4), scales=w_scales[w, a][:], in_=w_grouped[w, a][:]
+            )
+
+        def gather(u, plane):
+            a, i = divmod(plane, 4)
+            nc.vector.tensor_tensor(
+                picked[u, a][:, i, :],
+                planes[plane][:].indirect(lists[:, 32 * u : 32 * u + 32]),
+                weights[:, 512 * u : 512 * u + 512],
+                MULT,
+            )
+
+        def cast_x(u, a, half):
+            dst = x_grouped[u, a][:, 1024 * half : 1024 * half + 1024].rearrange("p (c i t) -> p c t i", i=4, t=4)
+            src = picked[u, a][:, :, 256 * half : 256 * half + 256].rearrange("p t (c i) -> p c t i", i=4)
+            cast("x%d%d%d" % (u, a, half), dst, src)
+
+        def quantize_x(u, a, half):
+            if "x%d%d" % (u, a) in SPLIT:
+                lo, hi = 256 * half, 256 * half + 256
+            elif half == 1:
+                lo, hi = 0, 512
+            else:
+                return
+            nc.vector.quantize_mx(
+                out=x_codes[u, a][:, lo:hi].bitcast(FP8X4),
+                scales=x_scales[u, a][:, lo:hi],
+                in_=x_grouped[u, a][:, 4 * lo : 4 * hi],
+            )
+
+        def product(w, kind, u, t, cols, acc):
             m = slice(128 * t, 128 * t + 128)
-            for a in range(2):
+            for step, a in enumerate(KORDER[kind]):
                 if w == "w2":
                     lhs = w2_codes[:, a, 256 * t : 256 * t + 256].bitcast(FP4X4)
                     lhs_scale = w2_planes[:, a, m]
@@ -162,95 +198,131 @@ def tile_list_triplet_contact_energy_kernel(
                     lhsT_scale=lhs_scale,
                     rhs=x_codes[u, a][:, cols].bitcast(FP8X4),
                     rhs_scale=x_scales[u, a][:, cols],
-                    start=(a == 0),
-                    stop=(a == 1),
+                    start=(step == 0),
+                    stop=(step == 1),
                 )
 
-        def stage_b(u):
-            n = UNITS[u]
-            b_sb[u] = keep.tile([P, 4, n], F32, name="b_sb_%d" % u)
-            w = 512 if n == 512 else 128
-            per = 512 // w
-            for c0 in range(0, n, w):
-                for g in range(4 // per):
-                    acc = psum.tile([P, per, w], F32, name="acc_b", bufs=NB[0])
-                    for t in range(per):
-                        product("w2", u, g * per + t, slice(c0, c0 + w), acc[:, t, :])
-                    nc.scalar.copy(out=b_sb[u][:, g * per : (g + 1) * per, c0 : c0 + w], in_=acc[:])
+        accs = {}
+        banks = [psum.tile([P, 512], F32, name="bank%d" % i, bufs=1) for i in range(8)]
 
-        def stage_c(u):
-            n = UNITS[u]
-            bc_sb[u] = b_sb[u]
-            per = 512 // n
-            for g in range(4 // per):
-                acc = psum.tile([P, per, n], F32, name="acc_c", bufs=NB[1])
-                for t in range(per):
-                    product("w3", u, g * per + t, slice(0, n), acc[:, t, :])
+        def next_bank(parts):
+            bank = banks[len(accs) % 8]
+            return bank[:].rearrange("p (t n) -> p t n", t=parts)
+
+        chunk = {}
+
+        def sum_b(u, t):
+            acc = next_bank(1)[:, 0, :]
+            product("w2", "b", u, t, slice(0, 512), acc)
+            accs["b", u, t] = acc
+
+        def stage_b(u, t):
+            acc = accs["b", u, t]
+            nc.scalar.copy(out=b_sb[u][:, t, :], in_=acc)
+
+        def sum_c(u, t):
+            acc = next_bank(1)[:, 0, :]
+            product("w3", "c", u, t, slice(0, 512), acc)
+            accs["c", u, t] = acc
+
+        def stage_c(u, t):
+            acc = accs["c", u, t]
+            nc.vector.scalar_tensor_tensor(
+                out=b_sb[u][:, t, :],
+                in0=acc,
+                scalar=b3_cols[:, t : t + 1],
+                in1=b_sb[u][:, t, :],
+                op0=ADD,
+                op1=MULT,
+            )
+
+        def sum_a(u, j):
+            cols = slice(128 * j, 128 * j + 128)
+            acc = next_bank(4)
+            for t in range(4):
+                product("w1", "a", u, t, cols, acc[:, t, :])
+            accs["a", u, j] = acc
+
+        def stage_a(u, j):
+            cols = slice(128 * j, 128 * j + 128)
+            acc = accs["a", u, j]
+            nc.vector.tensor_tensor(
+                h_tiles[u][:, 512 * j : 512 * j + 512].rearrange("p (c i t) -> p c t i", i=4, t=4),
+                acc.rearrange("p t (c i) -> p c t i", i=4),
+                b_sb[u][:, :, cols].rearrange("p t (c i) -> p c t i", i=4),
+                MULT,
+            )
+
+        def quantize_h(u, j):
+            if "e%d%d" % (u, j // 2) in SPLIT:
+                c0, ec = 128 * j, 128
+            else:
+                c0, ec = 128 * (j - 1), 256
+            h_codes = keep.tile([P, ec], U32, name="h_codes%d%d" % (u, j), align_bytes=64)
+            h_scales = keep.tile([P, ec], U8, name="h_scales%d%d" % (u, j), align_bytes=64)
+            nc.vector.quantize_mx(
+                out=h_codes[:].bitcast(FP8X4), scales=h_scales[:], in_=h_tiles[u][:, 4 * c0 : 4 * (c0 + ec)]
+            )
+            result = keep.tile([P, 4, ec], F32, name="result%d%d" % (u, j))
+            chunk[u, j] = (c0, ec, h_codes, h_scales, result)
+
+        def sum_e(u, j, g):
+            c0, ec, h_codes, h_scales, result = chunk[u, j]
+            per = 512 // ec
+            acc = next_bank(per)
+            for t in range(per):
+                m = slice(128 * (g * per + t), 128 * (g * per + t) + 128)
+                nc.tensor.matmul_mx(
+                    out=acc[:, t, :],
+                    lhsT=w4_codes[:, m].bitcast(FP8X4),
+                    lhsT_scale=given_scales[:, 2, m],
+                    rhs=h_codes[:].bitcast(FP8X4),
+                    rhs_scale=h_scales[:],
+                    start=True,
+                    stop=True,
+                )
+            accs["e", u, j, g] = acc
+
+        def add_bias(u, j, g):
+            c0, ec, h_codes, h_scales, result = chunk[u, j]
+            per = 512 // ec
+            acc = accs["e", u, j, g]
+            if "o%d%d%d" % (u, j, g) in VCAST:
+                nc.vector.tensor_tensor(
+                    result[:, g * per : (g + 1) * per, :],
+                    acc,
+                    b4_cols[:, g * per : (g + 1) * per].unsqueeze(2).to_broadcast([P, per, ec]),
+                    ADD,
+                )
+            else:
                 for t in range(per):
                     tt = g * per + t
-                    nc.vector.scalar_tensor_tensor(
-                        out=bc_sb[u][:, tt, :],
-                        in0=acc[:, t, :],
-                        scalar=b3_cols[:, tt : tt + 1],
-                        in1=b_sb[u][:, tt, :],
-                        op0=ADD,
-                        op1=MULT,
+                    nc.scalar.activation(
+                        out=result[:, tt, :], in_=acc[:, t, :], func=IDENT, bias=b4_cols[:, tt : tt + 1]
                     )
 
-        def stage_a(u):
-            n, s0 = UNITS[u], sum(UNITS[:u])
-            c0 = 0
-            for ec in ECH[u]:
-                h = ring.tile([P, 4 * ec], BF16, name="h", align_bytes=64)
-                for c in range(ec // 128):
-                    cols = slice(c0 + 128 * c, c0 + 128 * c + 128)
-                    acc = psum.tile([P, 4, 128], F32, name="acc_a", bufs=NB[2])
-                    for t in range(4):
-                        product("w1", u, t, cols, acc[:, t, :])
-                    nc.vector.tensor_tensor(
-                        h[:, 512 * c : 512 * c + 512].rearrange("p (c i t) -> p c t i", i=4, t=4),
-                        acc[:].rearrange("p t (c i) -> p c t i", i=4),
-                        bc_sb[u][:, :, cols].rearrange("p t (c i) -> p c t i", i=4),
-                        MULT,
-                    )
-                h_codes = ring.tile([P, ec], U32, name="h_codes", align_bytes=64)
-                h_scales = ring.tile([P, ec], U8, name="h_scales", align_bytes=64)
-                nc.vector.quantize_mx(out=h_codes[:].bitcast(FP8X4), scales=h_scales[:], in_=h[:])
-                result = ring.tile([P, 4, ec], F32, name="result")
-                per = 512 // ec
-                for g in range(4 // per):
-                    acc = psum.tile([P, per, ec], F32, name="acc_e", bufs=NB[3])
-                    for t in range(per):
-                        m = slice(128 * (g * per + t), 128 * (g * per + t) + 128)
-                        nc.tensor.matmul_mx(
-                            out=acc[:, t, :],
-                            lhsT=w4_codes[:, m].bitcast(FP8X4),
-                            lhsT_scale=given_scales[:, 2, m],
-                            rhs=h_codes[:].bitcast(FP8X4),
-                            rhs_scale=h_scales[:],
-                            start=True,
-                            stop=True,
-                        )
-                    for t in range(per):
-                        tt = g * per + t
-                        nc.scalar.activation(
-                            out=result[:, tt, :], in_=acc[:, t, :], func=IDENT, bias=b4_cols[:, tt : tt + 1]
-                        )
-                nc.sync.dma_start(
-                    out=out[:, s0 + c0 : s0 + c0 + ec].rearrange("(c p) j -> p c j", p=P), in_=result[:]
-                )
-                c0 += ec
+        def store(u, j):
+            c0, ec, h_codes, h_scales, result = chunk[u, j]
+            s0 = 512 * u + c0
+            nc.sync.dma_start(out=out[:, s0 : s0 + ec].rearrange("(c p) j -> p c j", p=P), in_=result[:])
 
+        steps = {
+            "P": permute_w2,
+            "G": gather,
+            "X": cast_x,
+            "Q": quantize_x,
+            "C": cast_weight,
+            "W": quantize_weight,
+            "b": stage_b,
+            "c": stage_c,
+            "A": stage_a,
+            "bm": sum_b,
+            "cm": sum_c,
+            "Am": sum_a,
+            "Eq": quantize_h,
+            "Em": sum_e,
+            "Eo": add_bias,
+            "Es": store,
+        }
         for step in PROG:
-            if step[0] == "P":
-                permute_w2()
-            elif step[0] == "W":
-                quantize_weight(step[1], step[2])
-            elif step[0] == "F":
-                gather(step[1], step[2])
-            elif step[0] == "b":
-                stage_b(step[1])
-            elif step[0] == "c":
-                stage_c(step[1])
-            else:
-                stage_a(step[1])
+            steps[step[0]](*step[1:])

@@ -19,13 +19,13 @@ IDENT = mybir.ActivationFunctionType.Identity
 
 P = 128
 UNITS = [512,512]
-REUSE = {"x01":"x00"}
+REUSE = {"w10":"x01"}
 Q2 = []
-SPLIT = ["e10","e11","x11"]
-KORDER = {"a":[0,1],"b":[0,1],"c":[0,1]}
-LOADS = ["s2","w2","offs","x3","g0","g1","x7","x0","x2","x1","x6","x4","w31","x5","w111","w30","w110","b3","w10","w4","s4","b4"]
-PROG = [["G",0,1],["C","w1",0,1],["G",0,4],["G",0,5],["C","w3",1,0],["G",1,5],["G",1,7],["G",0,6],["C","w1",1,0],["G",0,7],["C","w1",1,1],["G",1,6],["C","w3",0,1],["C","w1",0,0],["G",0,0],["G",0,2],["G",1,1],["G",1,3],["P"],["G",0,3],["X",0,0,0],["G",1,4],["G",1,0],["G",1,2],["X",0,0,1],["Q",0,0,1],["X",0,1,0],["X",1,0,0],["W","w1",1],["X",0,1,1],["C","w3",0,0],["W","w1",0],["Q",0,1,1],["X",1,0,1],["bm",0,0],["X",1,1,0],["W","w3",0],["Q",1,0,1],["bm",0,3],["bm",0,1],["C","w3",1,1],["bm",0,2],["W","w3",1],["b",0,0],["X",1,1,1],["Q",1,1,0],["Q",1,1,1],["b",0,1],["cm",0,3],["b",0,3],["bm",1,1],["bm",1,2],["b",0,2],["cm",0,2],["c",0,3],["cm",0,1],["cm",0,0],["b",1,1],["Am",0,1],["cm",1,2],["c",0,2],["cm",1,1],["b",1,2],["c",0,1],["c",0,0],["c",1,2],["Am",0,2],["Am",0,0],["Am",0,3],["bm",1,3],["A",0,3],["A",0,1],["bm",1,0],["A",0,0],["b",1,0],["c",1,1],["cm",1,3],["Eq",0,1],["A",0,2],["Em",0,1,0],["Em",0,1,1],["cm",1,0],["Am",1,0],["Am",1,1],["b",1,3],["Eo",0,1,0],["c",1,3],["c",1,0],["Eq",0,3],["Em",0,3,0],["A",1,0],["Eo",0,3,0],["Em",0,3,1],["Am",1,2],["Am",1,3],["A",1,3],["A",1,1],["A",1,2],["Eq",1,1],["Eo",0,1,1],["Eo",0,3,1],["Es",0,1],["Eq",1,0],["Em",1,0,0],["Eq",1,3],["Em",1,1,0],["Es",0,3],["Eo",1,1,0],["Eo",1,0,0],["Em",1,3,0],["Es",1,0],["Eo",1,3,0],["Eq",1,2],["Em",1,2,0],["Es",1,1],["Eo",1,2,0],["Es",1,2],["Es",1,3]]
-VCAST = ["o101","o110","o111","o120","o130","w110","w300","w301","x010"]
+SPLIT = ["e01","e10","e11","z10","z11","z12","z13"]
+KORDER = {"a":[1,0],"b":[0,1],"c":[0,1]}
+LOADS = ["w2","s2","x0","g0","offs","g1","x1","x2","x3","x4","x5","x6","w30","x7","w310","w101","b3","w311","w11","w100","s4","w4","b4"]
+PROG = [["P"],["G",0,0],["G",1,0],["G",0,1],["G",1,1],["G",0,2],["G",1,2],["G",0,3],["G",1,3],["G",0,4],["G",1,4],["G",0,5],["G",1,5],["G",0,6],["G",1,6],["G",0,7],["G",1,7],["X",0,0,0],["X",0,0,1],["Q",0,0,1],["C","w3",0,0],["C","w3",0,1],["W","w3",0],["X",0,1,0],["X",0,1,1],["Q",0,1,1],["C","w3",1,0],["C","w3",1,1],["W","w3",1],["bm",0,0],["cm",0,0],["bm",0,1],["cm",0,1],["bm",0,2],["cm",0,2],["bm",0,3],["cm",0,3],["X",1,0,0],["X",1,0,1],["Q",1,0,1],["X",1,1,0],["X",1,1,1],["Q",1,1,1],["C","w1",1,0],["C","w1",1,1],["C","w1",0,1],["C","w1",0,0],["W","w1",1],["W","w1",0],["b",0,0],["c",0,0],["b",0,1],["c",0,1],["b",0,2],["c",0,2],["b",0,3],["c",0,3],["bm",1,0],["cm",1,0],["bm",1,1],["cm",1,1],["Am",0,0],["Am",0,1],["b",1,0],["c",1,0],["b",1,1],["c",1,1],["bm",1,2],["cm",1,2],["A",0,0],["A",0,1],["Am",0,2],["Am",0,3],["bm",1,3],["cm",1,3],["b",1,2],["c",1,2],["Eq",0,1],["Em",0,1,0],["Em",0,1,1],["Eo",0,1,0],["Eo",0,1,1],["Es",0,1],["b",1,3],["c",1,3],["A",0,2],["A",0,3],["Am",1,0],["Am",1,1],["Eq",0,2],["Em",0,2,0],["Eo",0,2,0],["Es",0,2],["Eq",0,3],["Em",0,3,0],["Eo",0,3,0],["Es",0,3],["A",1,0],["A",1,1],["Am",1,2],["Am",1,3],["Eq",1,0],["Em",1,0,0],["Em",1,0,1],["Eo",1,0,0],["Eo",1,0,1],["Es",1,0],["A",1,2],["Eq",1,1],["Em",1,1,0],["Em",1,1,1],["Eo",1,1,0],["Eo",1,1,1],["Es",1,1],["A",1,3],["Eq",1,2],["Em",1,2,0],["Em",1,2,1],["Eo",1,2,0],["Eo",1,2,1],["Es",1,2],["Eq",1,3],["Em",1,3,0],["Em",1,3,1],["Eo",1,3,0],["Eo",1,3,1],["Es",1,3]]
+VCAST = ["w101","w110","w111","w311","x011","m10","m11","o111","o121","o131"]
 GCAST = []
 NB = [8]
 
@@ -227,6 +227,11 @@ def tile_list_triplet_contact_energy_kernel(
 
         def stage_c(u, t):
             acc = accs["c", u, t]
+            if "m%d%d" % (u, t) in VCAST:
+                shifted = picked[0, 0][:, t, :] if u == 0 else picked[1, 0][:, t, :]
+                nc.scalar.activation(out=shifted, in_=acc, func=IDENT, bias=b3_cols[:, t : t + 1])
+                nc.gpsimd.tensor_tensor(b_sb[u][:, t, :], shifted, b_sb[u][:, t, :], MULT)
+                return
             nc.vector.scalar_tensor_tensor(
                 out=b_sb[u][:, t, :],
                 in0=acc,
@@ -268,8 +273,8 @@ def tile_list_triplet_contact_energy_kernel(
 
         def sum_e(u, j, g):
             c0, ec, h_codes, h_scales, result = chunk[u, j]
-            per = 512 // ec
-            acc = next_bank(per)
+            per = 2 if "z%d%d" % (u, j) in SPLIT else 512 // ec
+            acc = next_bank(512 // ec)[:, 0:per, :]
             for t in range(per):
                 m = slice(128 * (g * per + t), 128 * (g * per + t) + 128)
                 nc.tensor.matmul_mx(
@@ -285,7 +290,7 @@ def tile_list_triplet_contact_energy_kernel(
 
         def add_bias(u, j, g):
             c0, ec, h_codes, h_scales, result = chunk[u, j]
-            per = 512 // ec
+            per = 2 if "z%d%d" % (u, j) in SPLIT else 512 // ec
             acc = accs["e", u, j, g]
             if "o%d%d%d" % (u, j, g) in VCAST:
                 nc.vector.tensor_tensor(

from contextlib import ExitStack

import concourse.mybir as mybir

K, T, S, H, N = 1024, 2048, 1024, 512, 512
FLOPS = 2 * S * (3 * K * H + H * N)

F32 = mybir.dt.float32
BF16 = mybir.dt.bfloat16
I32 = mybir.dt.int32
U32 = mybir.dt.uint32
U16 = mybir.dt.uint16
U8 = mybir.dt.uint8
FP8X4 = mybir.dt.float8_e4m3fn_x4
FP4X4 = mybir.dt.float4_e2m1fn_x4
MULT = mybir.AluOpType.mult
ADD = mybir.AluOpType.add
IDENT = mybir.ActivationFunctionType.Identity

P = 128
UNITS = [512,512]
REUSE = {"w10":"x01"}
Q2 = []
SPLIT = ["e01","e10","e11","z10","z11","z12","z13"]
KORDER = {"a":[1,0],"b":[0,1],"c":[0,1]}
LOADS = ["w2","s2","x0","g0","offs","g1","x1","x2","x3","x4","x5","x6","w30","x7","w310","w101","b3","w311","w11","w100","s4","w4","b4"]
PROG = [["P"],["G",0,0],["G",1,0],["G",0,1],["G",1,1],["G",0,2],["G",1,2],["G",0,3],["G",1,3],["G",0,4],["G",1,4],["G",0,5],["G",1,5],["G",0,6],["G",1,6],["G",0,7],["G",1,7],["X",0,0,0],["X",0,0,1],["Q",0,0,1],["C","w3",0,0],["C","w3",0,1],["W","w3",0],["X",0,1,0],["X",0,1,1],["Q",0,1,1],["C","w3",1,0],["C","w3",1,1],["W","w3",1],["bm",0,0],["cm",0,0],["bm",0,1],["cm",0,1],["bm",0,2],["cm",0,2],["bm",0,3],["cm",0,3],["X",1,0,0],["X",1,0,1],["Q",1,0,1],["X",1,1,0],["X",1,1,1],["Q",1,1,1],["C","w1",1,0],["C","w1",1,1],["C","w1",0,1],["C","w1",0,0],["W","w1",1],["W","w1",0],["b",0,0],["c",0,0],["b",0,1],["c",0,1],["b",0,2],["c",0,2],["b",0,3],["c",0,3],["bm",1,0],["cm",1,0],["bm",1,1],["cm",1,1],["Am",0,0],["Am",0,1],["b",1,0],["c",1,0],["b",1,1],["c",1,1],["bm",1,2],["cm",1,2],["A",0,0],["A",0,1],["Am",0,2],["Am",0,3],["bm",1,3],["cm",1,3],["b",1,2],["c",1,2],["Eq",0,1],["Em",0,1,0],["Em",0,1,1],["Eo",0,1,0],["Eo",0,1,1],["Es",0,1],["b",1,3],["c",1,3],["A",0,2],["A",0,3],["Am",1,0],["Am",1,1],["Eq",0,2],["Em",0,2,0],["Eo",0,2,0],["Es",0,2],["Eq",0,3],["Em",0,3,0],["Eo",0,3,0],["Es",0,3],["A",1,0],["A",1,1],["Am",1,2],["Am",1,3],["Eq",1,0],["Em",1,0,0],["Em",1,0,1],["Eo",1,0,0],["Eo",1,0,1],["Es",1,0],["A",1,2],["Eq",1,1],["Em",1,1,0],["Em",1,1,1],["Eo",1,1,0],["Eo",1,1,1],["Es",1,1],["A",1,3],["Eq",1,2],["Em",1,2,0],["Em",1,2,1],["Eo",1,2,0],["Eo",1,2,1],["Es",1,2],["Eq",1,3],["Em",1,3,0],["Em",1,3,1],["Eo",1,3,0],["Eo",1,3,1],["Es",1,3]]
VCAST = ["w101","w110","w111","w311","x011","m10","m11","o111","o121","o131"]
GCAST = []
NB = [8]


def tile_list_triplet_contact_energy_kernel(
    tc, xT, wgt, offs, w1, w2_words, w2_scales, w3, b3, w4_words, w4_scales, b4, out
):
    nc = tc.nc
    with ExitStack() as ctx:
        keep = ctx.enter_context(tc.tile_pool(name="keep", bufs=1))
        psum = ctx.enter_context(tc.psum_pool(name="psum", bufs=1))

        lists = keep.tile([P, S // 16], U16, name="lists")
        weights = keep.tile([P, S], F32, name="weights")
        planes = [keep.tile([P, T], F32, name="plane%d" % i) for i in range(8)]
        w_raw = {(w, a): keep.tile([P, 4, H], F32, name="raw_%s_%d" % (w, a)) for w in ("w1", "w3") for a in range(2)}
        w2_raw = keep.tile([P, 2, 2 * H], U8, name="w2_raw")
        given_scales = keep.tile([P, 3, H], U8, name="given_scales", align_bytes=64)
        w4_codes = keep.tile([P, N], U32, name="w4_codes", align_bytes=64)
        b3_cols = keep.tile([P, 4], F32, name="b3_cols")
        b4_cols = keep.tile([P, 4], F32, name="b4_cols")
        w2_codes = keep.tile([P, 2, 2 * H], U8, name="w2_codes", align_bytes=64)
        w2_planes = keep.tile([P, 2, H], U8, name="w2_planes", align_bytes=64)

        nc.vector.memset(given_scales[:].bitcast(U32), 0)
        src_w = {"w1": w1, "w3": w3}
        for name in LOADS:
            queue = nc.scalar if name in Q2 else nc.sync
            if name == "offs":
                nc.sync.dma_start(lists[:], offs)
            elif name[0] == "g":
                lo, hi = [(0, 512), (512, 1024)][int(name[1])]
                queue.dma_start(out=weights[:, lo:hi], in_=wgt[:, lo:hi])
            elif name[0] == "x":
                a, i = divmod(int(name[1]), 4)
                rows = xT[512 * a : 512 * (a + 1), :].rearrange("(p i) t -> p i t", i=4)
                queue.dma_start(out=planes[4 * a + i][:], in_=rows[:, i, :])
            elif name == "w2":
                queue.dma_start(out=w2_raw[:].bitcast(I32), in_=w2_words.rearrange("a p n -> p a n").bitcast(I32))
            elif name == "s2":
                for q in range(4):
                    queue.dma_start(
                        out=given_scales[32 * q : 32 * q + 4, 0:2, :].bitcast(I32),
                        in_=w2_scales[:, 4 * q : 4 * q + 4, :].rearrange("a q e -> q a e").bitcast(I32),
                    )
            elif name == "s4":
                for q in range(4):
                    queue.dma_start(
                        out=given_scales[32 * q : 32 * q + 4, 2, :].bitcast(I32),
                        in_=w4_scales[0, 4 * q : 4 * q + 4, :].bitcast(I32),
                    )
            elif name == "w4":
                queue.dma_start(
                    out=w4_codes[:].bitcast(I32), in_=w4_words[0].rearrange("p n t -> p (n t)").bitcast(I32)
                )
            elif name == "b3":
                queue.dma_start(out=b3_cols[:], in_=b3.rearrange("(p t) -> p t", t=4))
            elif name == "b4":
                with nc.allow_non_contiguous_dma(reason="one bias value a partition and output tile"):
                    queue.dma_start(out=b4_cols[:], in_=b4.rearrange("(c p) -> p c", p=P))
            else:
                w, a = name[:2], int(name[2])
                rows = src_w[w][512 * a : 512 * (a + 1), :].rearrange("(p j) c -> p j c", j=4)
                if len(name) == 3:
                    queue.dma_start(out=w_raw[w, a][:], in_=rows)
                else:
                    cols = slice(256 * int(name[3]), 256 * int(name[3]) + 256)
                    queue.dma_start(out=w_raw[w, a][:, :, cols], in_=rows[:, :, cols])

        w_codes = {}
        w_scales = {}
        x_codes = {}
        x_scales = {}
        b_sb = {}
        bc_sb = {}

        def permute_w2():
            for a in range(2):
                nc.vector.tensor_copy(
                    out=w2_codes[:, a, :].rearrange("p (t m b) -> p t m b", t=4, b=2),
                    in_=w2_raw[:, a, :].rearrange("p (m t b) -> p t m b", t=4, b=2),
                )
            nc.vector.tensor_copy(
                out=w2_planes[:].rearrange("p a (t m) -> p a t m", t=4),
                in_=given_scales[:, 0:2, :].rearrange("p a (m t) -> p a t m", t=4),
            )

        w_grouped = {}
        picked = {}
        x_grouped = {}
        h_tiles = {}
        staged = {}
        for key in ("x00", "x01", "x10", "x11", "w30", "w31", "w10", "w11"):
            if key not in REUSE:
                staged[key] = keep.tile([P, 2048], BF16, name="staged_" + key, align_bytes=64)
        for rounds in range(8):
            for key in REUSE:
                if REUSE[key] in staged:
                    staged[key] = staged[REUSE[key]]
        for key in w_raw:
            w_grouped[key] = staged["%s%d" % key]
            w_codes[key] = keep.tile([P, H], U32, name="codes_%s_%d" % key, align_bytes=64)
            w_scales[key] = keep.tile([P, H], U8, name="scales_%s_%d" % key, align_bytes=64)
        for u in range(2):
            b_sb[u] = keep.tile([P, 4, 512], F32, name="b_sb_%d" % u)
            h_tiles[u] = keep.tile([P, 2048], BF16, name="h_%d" % u, align_bytes=64)
            for a in range(2):
                picked[u, a] = keep.tile([P, 4, 512], F32, name="picked_%d_%d" % (u, a))
                x_grouped[u, a] = staged["x%d%d" % (u, a)]
                x_codes[u, a] = keep.tile([P, 512], U32, name="x_codes_%d_%d" % (u, a), align_bytes=64)
                x_scales[u, a] = keep.tile([P, 512], U8, name="x_scales_%d_%d" % (u, a), align_bytes=64)

        def cast(key, dst, src):
            if key in VCAST:
                nc.vector.tensor_copy(out=dst, in_=src)
            elif key in GCAST:
                nc.gpsimd.tensor_scalar(out=dst, in0=src, scalar1=1.0, scalar2=0.0, op0=MULT, op1=ADD)
            else:
                nc.scalar.copy(out=dst, in_=src)

        def cast_weight(w, a, half):
            dst = w_grouped[w, a][:].rearrange("p (t m j) -> p m j t", t=4, j=4)[:, 64 * half : 64 * half + 64]
            src = w_raw[w, a][:].rearrange("p j (m t) -> p m j t", t=4)[:, 64 * half : 64 * half + 64]
            cast("%s%d%d" % (w, a, half), dst, src)

        def quantize_weight(w, a):
            nc.vector.quantize_mx(
                out=w_codes[w, a][:].bitcast(FP8X4), scales=w_scales[w, a][:], in_=w_grouped[w, a][:]
            )

        def gather(u, plane):
            a, i = divmod(plane, 4)
            nc.vector.tensor_tensor(
                picked[u, a][:, i, :],
                planes[plane][:].indirect(lists[:, 32 * u : 32 * u + 32]),
                weights[:, 512 * u : 512 * u + 512],
                MULT,
            )

        def cast_x(u, a, half):
            dst = x_grouped[u, a][:, 1024 * half : 1024 * half + 1024].rearrange("p (c i t) -> p c t i", i=4, t=4)
            src = picked[u, a][:, :, 256 * half : 256 * half + 256].rearrange("p t (c i) -> p c t i", i=4)
            cast("x%d%d%d" % (u, a, half), dst, src)

        def quantize_x(u, a, half):
            if "x%d%d" % (u, a) in SPLIT:
                lo, hi = 256 * half, 256 * half + 256
            elif half == 1:
                lo, hi = 0, 512
            else:
                return
            nc.vector.quantize_mx(
                out=x_codes[u, a][:, lo:hi].bitcast(FP8X4),
                scales=x_scales[u, a][:, lo:hi],
                in_=x_grouped[u, a][:, 4 * lo : 4 * hi],
            )

        def product(w, kind, u, t, cols, acc):
            m = slice(128 * t, 128 * t + 128)
            for step, a in enumerate(KORDER[kind]):
                if w == "w2":
                    lhs = w2_codes[:, a, 256 * t : 256 * t + 256].bitcast(FP4X4)
                    lhs_scale = w2_planes[:, a, m]
                else:
                    lhs = w_codes[w, a][:, m].bitcast(FP8X4)
                    lhs_scale = w_scales[w, a][:, m]
                nc.tensor.matmul_mx(
                    out=acc,
                    lhsT=lhs,
                    lhsT_scale=lhs_scale,
                    rhs=x_codes[u, a][:, cols].bitcast(FP8X4),
                    rhs_scale=x_scales[u, a][:, cols],
                    start=(step == 0),
                    stop=(step == 1),
                )

        accs = {}
        banks = [psum.tile([P, 512], F32, name="bank%d" % i, bufs=1) for i in range(8)]

        def next_bank(parts):
            bank = banks[len(accs) % 8]
            return bank[:].rearrange("p (t n) -> p t n", t=parts)

        chunk = {}

        def sum_b(u, t):
            acc = next_bank(1)[:, 0, :]
            product("w2", "b", u, t, slice(0, 512), acc)
            accs["b", u, t] = acc

        def stage_b(u, t):
            acc = accs["b", u, t]
            nc.scalar.copy(out=b_sb[u][:, t, :], in_=acc)

        def sum_c(u, t):
            acc = next_bank(1)[:, 0, :]
            product("w3", "c", u, t, slice(0, 512), acc)
            accs["c", u, t] = acc

        def stage_c(u, t):
            acc = accs["c", u, t]
            if "m%d%d" % (u, t) in VCAST:
                shifted = picked[0, 0][:, t, :] if u == 0 else picked[1, 0][:, t, :]
                nc.scalar.activation(out=shifted, in_=acc, func=IDENT, bias=b3_cols[:, t : t + 1])
                nc.gpsimd.tensor_tensor(b_sb[u][:, t, :], shifted, b_sb[u][:, t, :], MULT)
                return
            nc.vector.scalar_tensor_tensor(
                out=b_sb[u][:, t, :],
                in0=acc,
                scalar=b3_cols[:, t : t + 1],
                in1=b_sb[u][:, t, :],
                op0=ADD,
                op1=MULT,
            )

        def sum_a(u, j):
            cols = slice(128 * j, 128 * j + 128)
            acc = next_bank(4)
            for t in range(4):
                product("w1", "a", u, t, cols, acc[:, t, :])
            accs["a", u, j] = acc

        def stage_a(u, j):
            cols = slice(128 * j, 128 * j + 128)
            acc = accs["a", u, j]
            nc.vector.tensor_tensor(
                h_tiles[u][:, 512 * j : 512 * j + 512].rearrange("p (c i t) -> p c t i", i=4, t=4),
                acc.rearrange("p t (c i) -> p c t i", i=4),
                b_sb[u][:, :, cols].rearrange("p t (c i) -> p c t i", i=4),
                MULT,
            )

        def quantize_h(u, j):
            if "e%d%d" % (u, j // 2) in SPLIT:
                c0, ec = 128 * j, 128
            else:
                c0, ec = 128 * (j - 1), 256
            h_codes = keep.tile([P, ec], U32, name="h_codes%d%d" % (u, j), align_bytes=64)
            h_scales = keep.tile([P, ec], U8, name="h_scales%d%d" % (u, j), align_bytes=64)
            nc.vector.quantize_mx(
                out=h_codes[:].bitcast(FP8X4), scales=h_scales[:], in_=h_tiles[u][:, 4 * c0 : 4 * (c0 + ec)]
            )
            result = keep.tile([P, 4, ec], F32, name="result%d%d" % (u, j))
            chunk[u, j] = (c0, ec, h_codes, h_scales, result)

        def sum_e(u, j, g):
            c0, ec, h_codes, h_scales, result = chunk[u, j]
            per = 2 if "z%d%d" % (u, j) in SPLIT else 512 // ec
            acc = next_bank(512 // ec)[:, 0:per, :]
            for t in range(per):
                m = slice(128 * (g * per + t), 128 * (g * per + t) + 128)
                nc.tensor.matmul_mx(
                    out=acc[:, t, :],
                    lhsT=w4_codes[:, m].bitcast(FP8X4),
                    lhsT_scale=given_scales[:, 2, m],
                    rhs=h_codes[:].bitcast(FP8X4),
                    rhs_scale=h_scales[:],
                    start=True,
                    stop=True,
                )
            accs["e", u, j, g] = acc

        def add_bias(u, j, g):
            c0, ec, h_codes, h_scales, result = chunk[u, j]
            per = 2 if "z%d%d" % (u, j) in SPLIT else 512 // ec
            acc = accs["e", u, j, g]
            if "o%d%d%d" % (u, j, g) in VCAST:
                nc.vector.tensor_tensor(
                    result[:, g * per : (g + 1) * per, :],
                    acc,
                    b4_cols[:, g * per : (g + 1) * per].unsqueeze(2).to_broadcast([P, per, ec]),
                    ADD,
                )
            else:
                for t in range(per):
                    tt = g * per + t
                    nc.scalar.activation(
                        out=result[:, tt, :], in_=acc[:, t, :], func=IDENT, bias=b4_cols[:, tt : tt + 1]
                    )

        def store(u, j):
            c0, ec, h_codes, h_scales, result = chunk[u, j]
            s0 = 512 * u + c0
            nc.sync.dma_start(out=out[:, s0 : s0 + ec].rearrange("(c p) j -> p c j", p=P), in_=result[:])

        steps = {
            "P": permute_w2,
            "G": gather,
            "X": cast_x,
            "Q": quantize_x,
            "C": cast_weight,
            "W": quantize_weight,
            "b": stage_b,
            "c": stage_c,
            "A": stage_a,
            "bm": sum_b,
            "cm": sum_c,
            "Am": sum_a,
            "Eq": quantize_h,
            "Em": sum_e,
            "Eo": add_bias,
            "Es": store,
        }
        for step in PROG:
            steps[step[0]](*step[1:])
